import numpy as np
import ml_dtypes


def mxq(x, axis, fmt="e4m3"):
    dtype, down = {"e4m3": (ml_dtypes.float8_e4m3fn, 7), "e5m2": (ml_dtypes.float8_e5m2, 14)}[fmt]
    v = np.moveaxis(np.asarray(x, np.float32).astype(ml_dtypes.bfloat16).astype(np.float64), axis, -1)
    blocks = v.reshape(v.shape[:-1] + (-1, 32))
    amax = np.abs(blocks).max(-1, keepdims=True)
    byte = np.maximum(np.where(amax > 0, np.frexp(amax)[1] - 1 + 127, 0) - down, 1)
    scale = np.exp2(byte - 127.0)
    codes = (blocks / scale).astype(np.float32).astype(dtype).astype(np.float64)
    return np.moveaxis((codes * scale).reshape(v.shape), -1, axis)


WIDE = False


def mx_kscale(k):
    if not WIDE:
        return np.ones(k)
    levels = np.array([10, -10, 5, -5, 0])
    if k % 512:
        return np.exp2(np.random.permutation(np.resize(levels, k // 32))).repeat(32)
    a = np.empty((k // 512, 16))
    for p in range(k // 512):
        a[p, :8] = np.random.permutation(np.resize(levels, 8))
        for g in range(8):
            far = levels[np.abs(levels - a[p, g]) >= 10]
            a[p, g + 8] = far[np.random.randint(len(far))]
    return np.exp2(a.ravel()).repeat(32)


def f64(x):
    return np.asarray(x).astype(np.float64)


def striped(idx):
    return np.tile(idx.reshape(-1, 16).T, (8, 1)).astype(np.uint16)


def unstriped(offs):
    return offs[:16].T.reshape(-1).astype(np.int64)


E2M1 = np.array([0.0, 0.5, 1.0, 1.5, 2.0, 3.0, 4.0, 6.0, -0.0, -0.5, -1.0, -1.5, -2.0, -3.0, -4.0, -6.0])


def pack_weight(w, fmt):
    k, n = w.shape
    w = f64(np.asarray(w, np.float32).astype(ml_dtypes.bfloat16)).reshape(k // 32, 32, n)
    amax = np.abs(w).max(1)
    if fmt == "e4m3":
        byte = np.frexp(amax)[1] - 1 + 127 - 7
    else:
        mant, ex = np.frexp(amax / 6.0)
        byte = np.where(mant > 0.5, ex, ex - 1) + 127
    byte = np.clip(np.where(amax > 0, byte, 1), 1, 254)
    scaled = (w * np.exp2(127.0 - byte)[:, None, :]).reshape(k, n).astype(np.float32)
    by_word = np.ascontiguousarray(scaled.reshape(k // 512, 128, 4, n).transpose(0, 1, 3, 2))
    if fmt == "e4m3":
        words = by_word.astype(ml_dtypes.float8_e4m3fn).view(np.uint8)
    else:
        c = by_word.astype(ml_dtypes.float4_e2m1fn).view(np.uint8) & 0xF
        words = (c[..., 0::2] | (c[..., 1::2] << 4)).reshape(k // 512, 128, 2 * n)
    return np.ascontiguousarray(words), np.ascontiguousarray(byte.astype(np.uint8).reshape(k // 512, 16, n))


def unpack_weight(words, scales, fmt):
    g, _, n = scales.shape
    words = np.ascontiguousarray(words).reshape(g, 128, n, -1)
    if fmt == "e4m3":
        vals = words.view(ml_dtypes.float8_e4m3fn).astype(np.float64)
    else:
        nib = np.empty((g, 128, n, 4), np.uint8)
        nib[..., 0::2] = words & 0xF
        nib[..., 1::2] = words >> 4
        vals = E2M1[nib]
    vals = vals * np.repeat(np.exp2(scales.astype(np.float64) - 127.0), 8, axis=1)[..., None]
    return vals.transpose(0, 1, 3, 2).reshape(g * 512, n)


def gelu(v):
    return 0.5 * v * (1.0 + np.tanh(np.sqrt(2.0 / np.pi) * (v + 0.044715 * v**3)))


def often(T, S):
    return np.random.permutation(T)[(T * np.random.uniform(0, 1, S) ** 4).astype(np.int64)]


K, K2, T, S, P, H, N = 1024, 512, 4096, 1024, 512, 512, 768


def setup_inputs():
    n = np.random.standard_normal
    s, s2, u = mx_kscale(K)[:, None], mx_kscale(K2)[:, None], mx_kscale(H)[:, None]
    d = {}
    d["tab_words"], d["tab_scales"] = pack_weight(n((K, T)) * s, "e4m3")
    d["tab2_words"], d["tab2_scales"] = pack_weight(n((K2, T)) * s2, "e4m3")
    d["tab3_words"], d["tab3_scales"] = pack_weight(n((K2, T)) * s2, "e4m3")
    d["offs"] = striped(np.random.permutation(T)[:S])
    d["offs2"] = striped(np.random.permutation(T)[:S])
    d["offs3"] = striped(np.random.permutation(T)[:S])
    d["pos1"] = striped(np.random.permutation(S)[:P])
    d["pos2"] = striped(often(S, P))
    d["pos3"] = striped(often(S, P))
    d["w1"] = (n((K, H)) / K ** 0.5 / s).astype(np.float32)
    d["w2_words"], d["w2_scales"] = pack_weight(0.8 * n((K2, H)) / K2 ** 0.5 / s2 * u.T, "e2m1")
    d["w3"] = (1.2 * n((K2, H)) / K2 ** 0.5 / s2 * u.T).astype(np.float32)
    d["w4"] = (n((H, N)) / H ** 0.5 / u).astype(np.float32)
    d["setting"] = n((H, S)).astype(np.float32)
    d["gain"] = (1.5 * np.exp(0.3 * n(H)) * u[:, 0]).astype(np.float32)
    return d


def reference(tab_words, tab_scales, tab2_words, tab2_scales, tab3_words, tab3_scales, offs, offs2, offs3,
              pos1, pos2, pos3, w1, w2_words, w2_scales, w3, w4, setting, gain):
    v = unpack_weight(tab_words, tab_scales, "e4m3")[:, unstriped(offs)]
    v2 = unpack_weight(tab2_words, tab2_scales, "e4m3")[:, unstriped(offs2)]
    v3 = unpack_weight(tab3_words, tab3_scales, "e4m3")[:, unstriped(offs3)]
    a = (mxq(f64(w1), 0, "e4m3").T @ v) + f64(setting)
    b = unpack_weight(w2_words, w2_scales, "e2m1").T @ v2
    d = mxq(f64(w3), 0, "e4m3").T @ v3
    x = f64(gain)[:, None] * np.tanh(a[:, unstriped(pos1)])
    z = np.maximum(x - b[:, unstriped(pos2)], d[:, unstriped(pos3)])
    return mxq(f64(w4), 0, "e4m3").T @ mxq(z, 0, "e4m3")

@@ -1,0 +1,286 @@
+from contextlib import ExitStack
+
+import concourse.mybir as mybir
+
+K, K2, T, S, PJ, H, N = 1024, 512, 4096, 1024, 512, 512, 768
+FLOPS = 2 * (K * H * S + 2 * K2 * H * S + H * N * PJ)
+
+F32 = mybir.dt.float32
+BF16 = mybir.dt.bfloat16
+I32 = mybir.dt.int32
+U32 = mybir.dt.uint32
+U16 = mybir.dt.uint16
+U8 = mybir.dt.uint8
+FP8X4 = mybir.dt.float8_e4m3fn_x4
+FP4X4 = mybir.dt.float4_e2m1fn_x4
+ALU = mybir.AluOpType
+ACT = mybir.ActivationFunctionType
+
+P = 128
+PACK = 4
+BANK = 512
+CHUNKS = (256, 256)
+
+
+def tile_list_tube_acceptance_features_kernel(
+    tc, tab_words, tab_scales, tab2_words, tab2_scales, tab3_words, tab3_scales, offs, offs2, offs3,
+    pos1, pos2, pos3, w1, w2_words, w2_scales, w3, w4, setting, gain, out,
+):
+    nc = tc.nc
+    with ExitStack() as ctx:
+        keep = ctx.enter_context(tc.tile_pool(name="keep", bufs=1))
+        big = ctx.enter_context(tc.tile_pool(name="big", bufs=1))
+        psum = ctx.enter_context(tc.psum_pool(name="psum", bufs=8))
+
+        def load_list(src, name):
+            lst = keep.tile([P, src.shape[1]], U16, name=name)
+            nc.sync.dma_start(lst[:], src)
+            return lst
+
+        def load_scale_rows(scales, name, tag):
+            passes = scales.shape[0]
+            first = P - 16 * passes
+            rows = big.tile([P, T], U8, name=name, tag=tag, align_bytes=64)
+            for a in range(passes):
+                nc.sync.dma_start(rows[first + a : P : passes, :].bitcast(I32), scales[a].bitcast(I32))
+            nc.vector.memset(rows[0:first, :].bitcast(I32), 0)
+            return rows
+
+        def place_scale_rows(picked, passes, name):
+            first = P - 16 * passes
+            plane = keep.tile([P, passes, S], U8, name=name, align_bytes=64)
+            nc.vector.memset(plane[:].rearrange("p a s -> p (a s)").bitcast(I32), 0)
+            for q in range(4):
+                nc.gpsimd.dma_start(
+                    plane[32 * q : 32 * q + 4, :, :].bitcast(I32),
+                    picked[first + 4 * passes * q : first + 4 * passes * (q + 1), :].bitcast(I32),
+                )
+            return plane
+
+        def load_words(words, name, tag):
+            win = big.tile([P, T], I32, name=name, tag=tag, align_bytes=64)
+            nc.sync.dma_start(win[:], words.rearrange("p t i -> p (t i)").bitcast(I32))
+            return win
+
+        def gather_scales(rows, lst, name):
+            picked = keep.tile([P, S], U8, name=name, align_bytes=64)
+            nc.vector.tensor_copy(picked[:], rows[:].indirect(lst[:]))
+            return picked
+
+        def gather_words(win, lst, name):
+            halves = []
+            for h in range(S // BANK):
+                picked = keep.tile([P, BANK], U32, name="%s_%d" % (name, h), align_bytes=64)
+                nc.vector.tensor_copy(picked[:], win[:].bitcast(U32).indirect(lst[:, 32 * h : 32 * h + 32]))
+                halves.append(picked)
+            return halves
+
+        def load_weight(rows, name, tag):
+            raw = big.tile([P, PACK, H], F32, name=name, tag=tag, align_bytes=64)
+            nc.sync.dma_start(raw[:], rows.rearrange("(p j) c -> p j c", j=PACK))
+            return raw
+
+        def round_weight(raw, name):
+            grouped = keep.tile([P, PACK * H], BF16, name=name, tag=name, align_bytes=64)
+            nc.scalar.copy(
+                grouped[:].rearrange("p (t g i j) -> p t g i j", t=4, g=16, i=8),
+                raw[:].rearrange("p j (g t i) -> p t g i j", t=4, i=8),
+            )
+            return grouped
+
+        def quantize(grouped, width, name):
+            codes = keep.tile([P, width], U32, name=name + "_codes", align_bytes=64)
+            plane = keep.tile([P, width], U8, name=name + "_plane", align_bytes=64)
+            c0 = 0
+            while c0 < width:
+                c1 = min(c0 + 512, width)
+                nc.vector.quantize_mx(
+                    out=codes[:, c0:c1].bitcast(FP8X4), scales=plane[:, c0:c1], in_=grouped[:, PACK * c0 : PACK * c1]
+                )
+                c0 = c1
+            return codes, plane
+
+        def dealt(rows, t):
+            return rows.rearrange("(g t i) c -> t g i c", t=4, i=8)[t]
+
+        w2s_rows = keep.tile([P, H], U8)
+        nc.vector.memset(w2s_rows[:].bitcast(I32), 0)
+        l2 = load_list(offs2, "l2")
+        s2_rows = load_scale_rows(tab2_scales, "s2_rows", "rows0")
+        l3 = load_list(offs3, "l3")
+        s3_rows = load_scale_rows(tab3_scales, "s3_rows", "rows1")
+        l1 = load_list(offs, "l1")
+        s1_rows = load_scale_rows(tab_scales, "s1_rows", "rows2")
+        w3_raw = load_weight(w3, "w3_raw", "raw0")
+        win2 = load_words(tab2_words[0], "win2", "win2")
+        for q in range(4):
+            nc.sync.dma_start(
+                w2s_rows[32 * q : 32 * q + 4, :].bitcast(I32), w2_scales[0, 4 * q : 4 * q + 4, :].bitcast(I32)
+            )
+        w2_raw = keep.tile([P, H // 2], I32)
+        nc.sync.dma_start(w2_raw[:], w2_words[0].bitcast(I32))
+        win3 = load_words(tab3_words[0], "win3", "win3")
+        w1_raw = [load_weight(w1[0:512, :], "w1_raw0", "raw1")]
+        p2 = load_list(pos2, "p2")
+        p3 = load_list(pos3, "p3")
+        w1_raw.append(load_weight(w1[512:1024, :], "w1_raw1", "raw2"))
+        win1 = [load_words(tab_words[a], "win1_%d" % a, "win1_%d" % a) for a in range(2)]
+        p1 = load_list(pos1, "p1")
+        w4_raw = keep.tile([P, 4, N], F32)
+        for t in range(4):
+            nc.sync.dma_start(w4_raw[:, t, :], dealt(w4, t))
+
+        gain_sb = keep.tile([P, 4, 8], F32)
+        with nc.allow_non_contiguous_dma(reason="one gain value per partition and slice"):
+            for t in range(4):
+                nc.sync.dma_start(gain_sb[:, t, 0:1], gain.rearrange("(g t i o) -> t g i o", t=4, i=8, o=1)[t])
+
+        warm_in = keep.tile([P, 1], F32)
+        nc.vector.memset(warm_in[:], 0.0)
+        warm_out = keep.tile([P, 1], F32)
+        nc.scalar.activation(warm_out[:], warm_in[:], ACT.Tanh)
+
+        g2s = place_scale_rows(gather_scales(s2_rows, l2, "pick2"), 1, "g2s")
+        g3s = place_scale_rows(gather_scales(s3_rows, l3, "pick3"), 1, "g3s")
+        g1s = place_scale_rows(gather_scales(s1_rows, l1, "pick1"), 2, "g1s")
+
+        w2_codes = keep.tile([P, 2 * H], U8, align_bytes=64)
+        nc.vector.tensor_copy(
+            w2_codes[:].bitcast(I32).rearrange("p (t g e) -> p t g e", t=4, e=4),
+            w2_raw[:].rearrange("p (g t e) -> p t g e", t=4, e=4),
+        )
+        w2_plane = keep.tile([P, H], U8, align_bytes=64)
+        nc.vector.tensor_copy(
+            w2_plane[:].bitcast(I32).rearrange("p (t g e) -> p t g e", t=4, e=2),
+            w2s_rows[:].bitcast(I32).rearrange("p (g t e) -> p t g e", t=4, e=2),
+        )
+        w3_bf = round_weight(w3_raw, "w3_bf")
+        w3_codes, w3_plane = quantize(w3_bf, H, "w3")
+        g2w = gather_words(win2, l2, "g2w")
+
+        setting_sb = big.tile([P, 4, S], F32, tag="win2", align_bytes=64)
+        for t in range(4):
+            nc.sync.dma_start(setting_sb[:, t, :], dealt(setting, t))
+
+        b_sb = [keep.tile([P, S], F32, name="b_sb%d" % t) for t in range(4)]
+        for t in range(4):
+            for h in range(2):
+                cols = slice(BANK * h, BANK * (h + 1))
+                acc = psum.tile([P, BANK], F32, tag="acc")
+                nc.tensor.matmul_mx(
+                    out=acc[:], lhsT=w2_codes[:, 2 * P * t : 2 * P * (t + 1)].bitcast(FP4X4),
+                    lhsT_scale=w2_plane[:, P * t : P * (t + 1)],
+                    rhs=g2w[h][:].bitcast(FP8X4), rhs_scale=g2s[:, 0, cols], start=True, stop=True,
+                )
+                nc.scalar.copy(b_sb[t][:, cols], acc[:])
+
+        g3w = gather_words(win3, l3, "g3w")
+
+        gbd = big.tile([P, 8, PJ], F32, tag="win3", align_bytes=64)
+        gb = gbd[:, 0:4, :]
+        gd = gbd[:, 4:8, :]
+        for t in range(4):
+            nc.vector.tensor_copy(gb[:, t, :], b_sb[t][:].indirect(p2[:]))
+
+        d_sb = [keep.tile([P, S], F32, name="d_sb%d" % t) for t in range(4)]
+        for t in range(4):
+            for h in range(2):
+                cols = slice(BANK * h, BANK * (h + 1))
+                acc = psum.tile([P, BANK], F32, tag="acc")
+                nc.tensor.matmul_mx(
+                    out=acc[:], lhsT=w3_codes[:, P * t : P * (t + 1)].bitcast(FP8X4),
+                    lhsT_scale=w3_plane[:, P * t : P * (t + 1)],
+                    rhs=g3w[h][:].bitcast(FP8X4), rhs_scale=g3s[:, 0, cols], start=True, stop=True,
+                )
+                nc.scalar.copy(d_sb[t][:, cols], acc[:])
+        w1_bf = [round_weight(w1_raw[a], "w1_bf%d" % a) for a in range(2)]
+        for t in range(4):
+            nc.vector.tensor_copy(gd[:, t, :], d_sb[t][:].indirect(p3[:]))
+
+        w1_q = [quantize(w1_bf[a], H, "w1_%d" % a) for a in range(2)]
+        accs = [[psum.tile([P, BANK], F32, tag="acc", name="acc") for t in range(4)] for h in range(2)]
+        for a in range(2):
+            g1w = gather_words(win1[a], l1, "g1w%d" % a)
+            codes, plane = w1_q[a]
+            for h in range(2):
+                for t in range(4):
+                    nc.tensor.matmul_mx(
+                        out=accs[h][t][:], lhsT=codes[:, P * t : P * (t + 1)].bitcast(FP8X4),
+                        lhsT_scale=plane[:, P * t : P * (t + 1)],
+                        rhs=g1w[h][:].bitcast(FP8X4),
+                        rhs_scale=g1s[:, a, BANK * h : BANK * (h + 1)],
+                        start=(a == 0), stop=(a == 1),
+                    )
+        a_sb = [big.tile([P, S], F32, name="a_sb%d" % t, tag="rows%d" % t, align_bytes=64) for t in range(4)]
+        for h in range(2):
+            cols = slice(BANK * h, BANK * (h + 1))
+            for t in range(4):
+                nc.vector.tensor_tensor(a_sb[t][:, cols], accs[h][t][:], setting_sb[:, t, cols], ALU.add)
+
+        w4_bf = keep.tile([P, PACK * N], BF16, align_bytes=64)
+        nc.scalar.copy(w4_bf[:].rearrange("p (n t) -> p n t", t=4), w4_raw[:].rearrange("p t n -> p n t"))
+
+        starts = [sum(CHUNKS[:c]) for c in range(len(CHUNKS))]
+        ga = []
+        for c, width in enumerate(CHUNKS):
+            picked = keep.tile([P, 4, width], F32, name="ga%d" % c)
+            for t in range(4):
+                nc.vector.tensor_copy(
+                    picked[:, t, :], a_sb[t][:].indirect(p1[:, starts[c] // 16 : (starts[c] + width) // 16])
+                )
+                nc.scalar.activation(picked[:, t, :], picked[:, t, :], ACT.Tanh)
+            ga.append(picked)
+        w4_codes, w4_plane = quantize(w4_bf, N, "w4")
+
+        out_v = out.rearrange("(n p) j -> p n j", p=P)
+        last = len(CHUNKS) - 1
+
+        def combine(c):
+            cols = slice(starts[c], starts[c] + CHUNKS[c])
+            for t in range(4):
+                nc.vector.scalar_tensor_tensor(
+                    ga[c][:, t, :], ga[c][:, t, :], gain_sb[:, t, 0:1], gb[:, t, cols], ALU.mult, ALU.subtract
+                )
+
+        def round_z(c):
+            width = CHUNKS[c]
+            cols = slice(starts[c], starts[c] + width)
+            z_bf = keep.tile([P, 4, width], BF16, name="z_bf%d" % c)
+            nc.vector.tensor_tensor(z_bf[:], ga[c][:], gd[:, :, cols], ALU.max)
+            grouped = keep.tile([P, PACK * width], BF16, name="z_il%d" % c, align_bytes=64)
+            src = z_bf[:].rearrange("p t j -> p j t")
+            dst = grouped[:].rearrange("p (j t) -> p j t", t=4)
+            if c < last:
+                nc.scalar.copy(dst, src)
+            else:
+                nc.vector.tensor_copy(dst, src)
+            return grouped
+
+        def project(c, grouped):
+            width = CHUNKS[c]
+            cols = slice(starts[c], starts[c] + width)
+            z_codes, z_plane = quantize(grouped, width, "z%d" % c)
+            per_bank = min(BANK // width, 2)
+            staged = big.tile([P, N // P, width], F32, name="staged", tag="raw%d" % c, align_bytes=64)
+            for n0 in range(0, N // P, per_bank):
+                acc = psum.tile([P, per_bank, width], F32, tag="acc")
+                for i in range(per_bank):
+                    n = n0 + i
+                    nc.tensor.matmul_mx(
+                        out=acc[:, i, :], lhsT=w4_codes[:, P * n : P * (n + 1)].bitcast(FP8X4),
+                        lhsT_scale=w4_plane[:, P * n : P * (n + 1)],
+                        rhs=z_codes[:].bitcast(FP8X4), rhs_scale=z_plane[:], start=True, stop=True,
+                    )
+                if c == last and (n0 // per_bank) % 2 == 1:
+                    nc.vector.tensor_copy(staged[:, n0 : n0 + per_bank, :], acc[:])
+                else:
+                    nc.scalar.copy(staged[:, n0 : n0 + per_bank, :], acc[:])
+                nc.sync.dma_start(out_v[:, n0 : n0 + per_bank, cols], staged[:, n0 : n0 + per_bank, :])
+
+        combine(0)
+        grouped = round_z(0)
+        for c in range(1, len(CHUNKS)):
+            combine(c)
+            project(c - 1, grouped)
+            grouped = round_z(c)
+        project(last, grouped)

@@ -19,7 +19,7 @@ ACT = mybir.ActivationFunctionType
 P = 128
 PACK = 4
 BANK = 512
-CHUNKS = (256, 256)
+CHUNKS = (256, 128, 128)
 
 
 def tile_list_tube_acceptance_features_kernel(
@@ -51,7 +51,7 @@ def tile_list_tube_acceptance_features_kernel(
             plane = keep.tile([P, passes, S], U8, name=name, align_bytes=64)
             nc.vector.memset(plane[:].rearrange("p a s -> p (a s)").bitcast(I32), 0)
             for q in range(4):
-                nc.gpsimd.dma_start(
+                nc.sync.dma_start(
                     plane[32 * q : 32 * q + 4, :, :].bitcast(I32),
                     picked[first + 4 * passes * q : first + 4 * passes * (q + 1), :].bitcast(I32),
                 )
@@ -70,7 +70,7 @@ def tile_list_tube_acceptance_features_kernel(
         def gather_words(win, lst, name):
             halves = []
             for h in range(S // BANK):
-                picked = keep.tile([P, BANK], U32, name="%s_%d" % (name, h), align_bytes=64)
+                picked = keep.tile([P, BANK], U32, name="picked", tag="%s_%d" % (name, h), align_bytes=64)
                 nc.vector.tensor_copy(picked[:], win[:].bitcast(U32).indirect(lst[:, 32 * h : 32 * h + 32]))
                 halves.append(picked)
             return halves
@@ -80,8 +80,8 @@ def tile_list_tube_acceptance_features_kernel(
             nc.sync.dma_start(raw[:], rows.rearrange("(p j) c -> p j c", j=PACK))
             return raw
 
-        def round_weight(raw, name):
-            grouped = keep.tile([P, PACK * H], BF16, name=name, tag=name, align_bytes=64)
+        def round_weight(raw, tag):
+            grouped = keep.tile([P, PACK * H], BF16, tag=tag, align_bytes=64)
             nc.scalar.copy(
                 grouped[:].rearrange("p (t g i j) -> p t g i j", t=4, g=16, i=8),
                 raw[:].rearrange("p j (g t i) -> p t g i j", t=4, i=8),
@@ -106,34 +106,22 @@ def tile_list_tube_acceptance_features_kernel(
         w2s_rows = keep.tile([P, H], U8)
         nc.vector.memset(w2s_rows[:].bitcast(I32), 0)
         l2 = load_list(offs2, "l2")
-        s2_rows = load_scale_rows(tab2_scales, "s2_rows", "rows0")
+        s2_rows = load_scale_rows(tab2_scales, "s2_rows", "slot_a")
         l3 = load_list(offs3, "l3")
-        s3_rows = load_scale_rows(tab3_scales, "s3_rows", "rows1")
+        s3_rows = load_scale_rows(tab3_scales, "s3_rows", "slot_b")
         l1 = load_list(offs, "l1")
-        s1_rows = load_scale_rows(tab_scales, "s1_rows", "rows2")
-        w3_raw = load_weight(w3, "w3_raw", "raw0")
-        win2 = load_words(tab2_words[0], "win2", "win2")
+        s1_rows = load_scale_rows(tab_scales, "s1_rows", "slot_c")
+        w3_raw = load_weight(w3, "w3_raw", "slot_d")
         for q in range(4):
             nc.sync.dma_start(
                 w2s_rows[32 * q : 32 * q + 4, :].bitcast(I32), w2_scales[0, 4 * q : 4 * q + 4, :].bitcast(I32)
             )
         w2_raw = keep.tile([P, H // 2], I32)
         nc.sync.dma_start(w2_raw[:], w2_words[0].bitcast(I32))
-        win3 = load_words(tab3_words[0], "win3", "win3")
-        w1_raw = [load_weight(w1[0:512, :], "w1_raw0", "raw1")]
+        p1 = load_list(pos1, "p1")
+        win2 = load_words(tab2_words[0], "win2", "slot_e")
         p2 = load_list(pos2, "p2")
         p3 = load_list(pos3, "p3")
-        w1_raw.append(load_weight(w1[512:1024, :], "w1_raw1", "raw2"))
-        win1 = [load_words(tab_words[a], "win1_%d" % a, "win1_%d" % a) for a in range(2)]
-        p1 = load_list(pos1, "p1")
-        w4_raw = keep.tile([P, 4, N], F32)
-        for t in range(4):
-            nc.sync.dma_start(w4_raw[:, t, :], dealt(w4, t))
-
-        gain_sb = keep.tile([P, 4, 8], F32)
-        with nc.allow_non_contiguous_dma(reason="one gain value per partition and slice"):
-            for t in range(4):
-                nc.sync.dma_start(gain_sb[:, t, 0:1], gain.rearrange("(g t i o) -> t g i o", t=4, i=8, o=1)[t])
 
         warm_in = keep.tile([P, 1], F32)
         nc.vector.memset(warm_in[:], 0.0)
@@ -141,10 +129,13 @@ def tile_list_tube_acceptance_features_kernel(
         nc.scalar.activation(warm_out[:], warm_in[:], ACT.Tanh)
 
         g2s = place_scale_rows(gather_scales(s2_rows, l2, "pick2"), 1, "g2s")
+        win3 = load_words(tab3_words[0], "win3", "slot_a")
         g3s = place_scale_rows(gather_scales(s3_rows, l3, "pick3"), 1, "g3s")
+        w1_raw = [load_weight(w1[0:512, :], "w1_raw0", "slot_b")]
         g1s = place_scale_rows(gather_scales(s1_rows, l1, "pick1"), 2, "g1s")
+        w1_raw.append(load_weight(w1[512:1024, :], "w1_raw1", "slot_c"))
 
-        w2_codes = keep.tile([P, 2 * H], U8, align_bytes=64)
+        w2_codes = big.tile([P, 2 * H], U8, tag="slot_f", align_bytes=64)
         nc.vector.tensor_copy(
             w2_codes[:].bitcast(I32).rearrange("p (t g e) -> p t g e", t=4, e=4),
             w2_raw[:].rearrange("p (g t e) -> p t g e", t=4, e=4),
@@ -155,14 +146,18 @@ def tile_list_tube_acceptance_features_kernel(
             w2s_rows[:].bitcast(I32).rearrange("p (g t e) -> p t g e", t=4, e=2),
         )
         w3_bf = round_weight(w3_raw, "w3_bf")
+        win1 = [load_words(tab_words[0], "win1_0", "slot_d")]
         w3_codes, w3_plane = quantize(w3_bf, H, "w3")
+        gain_sb = keep.tile([P, 4, 8], F32, tag="w3_bf", align_bytes=64)
+        with nc.allow_non_contiguous_dma(reason="one gain value per partition and slice"):
+            for t in range(4):
+                nc.sync.dma_start(gain_sb[:, t, 0:1], gain.rearrange("(g t i o) -> t g i o", t=4, i=8, o=1)[t])
+
         g2w = gather_words(win2, l2, "g2w")
 
-        setting_sb = big.tile([P, 4, S], F32, tag="win2", align_bytes=64)
-        for t in range(4):
-            nc.sync.dma_start(setting_sb[:, t, :], dealt(setting, t))
+        win1.append(load_words(tab_words[1], "win1_1", "slot_e"))
 
-        b_sb = [keep.tile([P, S], F32, name="b_sb%d" % t) for t in range(4)]
+        b_sb = [big.tile([P, S], F32, name="b_sb%d" % t, tag="slot_g%d" % t) for t in range(4)]
         for t in range(4):
             for h in range(2):
                 cols = slice(BANK * h, BANK * (h + 1))
@@ -174,13 +169,20 @@ def tile_list_tube_acceptance_features_kernel(
                 )
                 nc.scalar.copy(b_sb[t][:, cols], acc[:])
 
+        w4_raw = big.tile([P, 4, N], F32, tag="slot_f", align_bytes=64)
+        for t in range(4):
+            nc.sync.dma_start(w4_raw[:, t, :], dealt(w4, t))
+
         g3w = gather_words(win3, l3, "g3w")
 
-        gbd = big.tile([P, 8, PJ], F32, tag="win3", align_bytes=64)
+        gbd = big.tile([P, 8, PJ], F32, tag="slot_a", align_bytes=64)
         gb = gbd[:, 0:4, :]
         gd = gbd[:, 4:8, :]
         for t in range(4):
             nc.vector.tensor_copy(gb[:, t, :], b_sb[t][:].indirect(p2[:]))
+        setting_sb = [big.tile([P, S], F32, name="setting%d" % t, tag="slot_g%d" % t) for t in range(4)]
+        for t in range(4):
+            nc.sync.dma_start(setting_sb[t][:], dealt(setting, t))
 
         d_sb = [keep.tile([P, S], F32, name="d_sb%d" % t) for t in range(4)]
         for t in range(4):
@@ -193,7 +195,7 @@ def tile_list_tube_acceptance_features_kernel(
                     rhs=g3w[h][:].bitcast(FP8X4), rhs_scale=g3s[:, 0, cols], start=True, stop=True,
                 )
                 nc.scalar.copy(d_sb[t][:, cols], acc[:])
-        w1_bf = [round_weight(w1_raw[a], "w1_bf%d" % a) for a in range(2)]
+        w1_bf = [round_weight(w1_raw[a], "g3w_%d" % (1 - a)) for a in range(2)]
         for t in range(4):
             nc.vector.tensor_copy(gd[:, t, :], d_sb[t][:].indirect(p3[:]))
 
@@ -211,11 +213,11 @@ def tile_list_tube_acceptance_features_kernel(
                         rhs_scale=g1s[:, a, BANK * h : BANK * (h + 1)],
                         start=(a == 0), stop=(a == 1),
                     )
-        a_sb = [big.tile([P, S], F32, name="a_sb%d" % t, tag="rows%d" % t, align_bytes=64) for t in range(4)]
-        for h in range(2):
-            cols = slice(BANK * h, BANK * (h + 1))
-            for t in range(4):
-                nc.vector.tensor_tensor(a_sb[t][:, cols], accs[h][t][:], setting_sb[:, t, cols], ALU.add)
+        a_sb = [keep.tile([P, S], F32, name="a_sb%d" % t) for t in range(4)]
+        for t in range(4):
+            for h in range(2):
+                cols = slice(BANK * h, BANK * (h + 1))
+                nc.vector.tensor_tensor(a_sb[t][:, cols], accs[h][t][:], setting_sb[t][:, cols], ALU.add)
 
         w4_bf = keep.tile([P, PACK * N], BF16, align_bytes=64)
         nc.scalar.copy(w4_bf[:].rearrange("p (n t) -> p n t", t=4), w4_raw[:].rearrange("p t n -> p n t"))
@@ -230,7 +232,6 @@ def tile_list_tube_acceptance_features_kernel(
                 )
                 nc.scalar.activation(picked[:, t, :], picked[:, t, :], ACT.Tanh)
             ga.append(picked)
-        w4_codes, w4_plane = quantize(w4_bf, N, "w4")
 
         out_v = out.rearrange("(n p) j -> p n j", p=P)
         last = len(CHUNKS) - 1
@@ -247,10 +248,13 @@ def tile_list_tube_acceptance_features_kernel(
             cols = slice(starts[c], starts[c] + width)
             z_bf = keep.tile([P, 4, width], BF16, name="z_bf%d" % c)
             nc.vector.tensor_tensor(z_bf[:], ga[c][:], gd[:, :, cols], ALU.max)
-            grouped = keep.tile([P, PACK * width], BF16, name="z_il%d" % c, align_bytes=64)
+            return z_bf
+
+        def weave_z(c, z_bf):
+            grouped = keep.tile([P, PACK * CHUNKS[c]], BF16, name="z_il%d" % c, align_bytes=64)
             src = z_bf[:].rearrange("p t j -> p j t")
             dst = grouped[:].rearrange("p (j t) -> p j t", t=4)
-            if c < last:
+            if c == 0:
                 nc.scalar.copy(dst, src)
             else:
                 nc.vector.tensor_copy(dst, src)
@@ -260,8 +264,8 @@ def tile_list_tube_acceptance_features_kernel(
             width = CHUNKS[c]
             cols = slice(starts[c], starts[c] + width)
             z_codes, z_plane = quantize(grouped, width, "z%d" % c)
-            per_bank = min(BANK // width, 2)
-            staged = big.tile([P, N // P, width], F32, name="staged", tag="raw%d" % c, align_bytes=64)
+            per_bank = min(BANK // width, 3)
+            staged = big.tile([P, N // P, width], F32, name="staged", tag=("slot_b", "slot_c", "slot_d")[c], align_bytes=64)
             for n0 in range(0, N // P, per_bank):
                 acc = psum.tile([P, per_bank, width], F32, tag="acc")
                 for i in range(per_bank):
@@ -278,9 +282,13 @@ def tile_list_tube_acceptance_features_kernel(
                 nc.sync.dma_start(out_v[:, n0 : n0 + per_bank, cols], staged[:, n0 : n0 + per_bank, :])
 
         combine(0)
-        grouped = round_z(0)
+        grouped = weave_z(0, round_z(0))
+        combine(1)
+        w4_codes, w4_plane = quantize(w4_bf, N, "w4")
         for c in range(1, len(CHUNKS)):
-            combine(c)
             project(c - 1, grouped)
-            grouped = round_z(c)
+            z_bf = round_z(c)
+            if c < last:
+                combine(c + 1)
+            grouped = weave_z(c, z_bf)
         project(last, grouped)

@@ -19,7 +19,7 @@ ACT = mybir.ActivationFunctionType
 P = 128
 PACK = 4
 BANK = 512
-CHUNKS = (256, 128, 128)
+CHUNKS = (128, 256, 128)
 
 
 def tile_list_tube_acceptance_features_kernel(
@@ -83,8 +83,8 @@ def tile_list_tube_acceptance_features_kernel(
         def round_weight(raw, tag):
             grouped = keep.tile([P, PACK * H], BF16, tag=tag, align_bytes=64)
             nc.scalar.copy(
-                grouped[:].rearrange("p (t g i j) -> p t g i j", t=4, g=16, i=8),
-                raw[:].rearrange("p j (g t i) -> p t g i j", t=4, i=8),
+                grouped[:].rearrange("p (t m j) -> p m j t", t=4, j=4),
+                raw[:].rearrange("p j (m t) -> p m j t", t=4),
             )
             return grouped
 
@@ -99,9 +99,6 @@ def tile_list_tube_acceptance_features_kernel(
                 )
                 c0 = c1
             return codes, plane
-
-        def dealt(rows, t):
-            return rows.rearrange("(g t i) c -> t g i c", t=4, i=8)[t]
 
         w2s_rows = keep.tile([P, H], U8)
         nc.vector.memset(w2s_rows[:].bitcast(I32), 0)
@@ -137,22 +134,17 @@ def tile_list_tube_acceptance_features_kernel(
 
         w2_codes = big.tile([P, 2 * H], U8, tag="slot_f", align_bytes=64)
         nc.vector.tensor_copy(
-            w2_codes[:].bitcast(I32).rearrange("p (t g e) -> p t g e", t=4, e=4),
-            w2_raw[:].rearrange("p (g t e) -> p t g e", t=4, e=4),
+            w2_codes[:].rearrange("p (t m e) -> p t m e", t=4, e=2),
+            w2_raw[:].bitcast(U8).rearrange("p (m t e) -> p t m e", t=4, e=2),
         )
         w2_plane = keep.tile([P, H], U8, align_bytes=64)
         nc.vector.tensor_copy(
-            w2_plane[:].bitcast(I32).rearrange("p (t g e) -> p t g e", t=4, e=2),
-            w2s_rows[:].bitcast(I32).rearrange("p (g t e) -> p t g e", t=4, e=2),
+            w2_plane[:].rearrange("p (t m) -> p t m", t=4),
+            w2s_rows[:].rearrange("p (m t) -> p t m", t=4),
         )
         w3_bf = round_weight(w3_raw, "w3_bf")
         win1 = [load_words(tab_words[0], "win1_0", "slot_d")]
         w3_codes, w3_plane = quantize(w3_bf, H, "w3")
-        gain_sb = keep.tile([P, 4, 8], F32, tag="w3_bf", align_bytes=64)
-        with nc.allow_non_contiguous_dma(reason="one gain value per partition and slice"):
-            for t in range(4):
-                nc.sync.dma_start(gain_sb[:, t, 0:1], gain.rearrange("(g t i o) -> t g i o", t=4, i=8, o=1)[t])
-
         g2w = gather_words(win2, l2, "g2w")
 
         win1.append(load_words(tab_words[1], "win1_1", "slot_e"))
@@ -170,8 +162,7 @@ def tile_list_tube_acceptance_features_kernel(
                 nc.scalar.copy(b_sb[t][:, cols], acc[:])
 
         w4_raw = big.tile([P, 4, N], F32, tag="slot_f", align_bytes=64)
-        for t in range(4):
-            nc.sync.dma_start(w4_raw[:, t, :], dealt(w4, t))
+        nc.sync.dma_start(w4_raw[:], w4.rearrange("(p t) n -> p t n", t=4))
 
         g3w = gather_words(win3, l3, "g3w")
 
@@ -180,9 +171,11 @@ def tile_list_tube_acceptance_features_kernel(
         gd = gbd[:, 4:8, :]
         for t in range(4):
             nc.vector.tensor_copy(gb[:, t, :], b_sb[t][:].indirect(p2[:]))
+        gain_sb = keep.tile([P, 4], F32, tag="w3_bf", align_bytes=64)
+        nc.sync.dma_start(gain_sb[:], gain.rearrange("(p t) -> p t", t=4))
         setting_sb = [big.tile([P, S], F32, name="setting%d" % t, tag="slot_g%d" % t) for t in range(4)]
         for t in range(4):
-            nc.sync.dma_start(setting_sb[t][:], dealt(setting, t))
+            nc.sync.dma_start(setting_sb[t][:], setting.rearrange("(p t) j -> t p j", t=4)[t])
 
         d_sb = [keep.tile([P, S], F32, name="d_sb%d" % t) for t in range(4)]
         for t in range(4):
@@ -213,56 +206,38 @@ def tile_list_tube_acceptance_features_kernel(
                         rhs_scale=g1s[:, a, BANK * h : BANK * (h + 1)],
                         start=(a == 0), stop=(a == 1),
                     )
-        a_sb = [keep.tile([P, S], F32, name="a_sb%d" % t) for t in range(4)]
+        w4_bf = keep.tile([P, PACK * N], BF16, align_bytes=64)
+        nc.scalar.copy(
+            w4_bf[:].rearrange("p (c e t) -> p c t e", e=4, t=4), w4_raw[:].rearrange("p t (c e) -> p c t e", e=4)
+        )
+        w4_codes, w4_plane = quantize(w4_bf, N, "w4")
+
+        x_sb = [keep.tile([P, S], F32, name="x_sb%d" % t) for t in range(4)]
         for t in range(4):
             for h in range(2):
                 cols = slice(BANK * h, BANK * (h + 1))
-                nc.vector.tensor_tensor(a_sb[t][:, cols], accs[h][t][:], setting_sb[t][:, cols], ALU.add)
+                nc.vector.tensor_tensor(x_sb[t][:, cols], accs[h][t][:], setting_sb[t][:, cols], ALU.add)
+                nc.scalar.activation(x_sb[t][:, cols], x_sb[t][:, cols], ACT.Tanh)
+                nc.scalar.activation(x_sb[t][:, cols], x_sb[t][:, cols], ACT.Copy, scale=gain_sb[:, t : t + 1])
 
-        w4_bf = keep.tile([P, PACK * N], BF16, align_bytes=64)
-        nc.scalar.copy(w4_bf[:].rearrange("p (n t) -> p n t", t=4), w4_raw[:].rearrange("p t n -> p n t"))
+        y = keep.tile([P, 4, PJ], F32)
+        z_bf = keep.tile([P, 4, PJ], BF16)
 
-        starts = [sum(CHUNKS[:c]) for c in range(len(CHUNKS))]
-        ga = []
-        for c, width in enumerate(CHUNKS):
-            picked = keep.tile([P, 4, width], F32, name="ga%d" % c)
-            for t in range(4):
-                nc.vector.tensor_copy(
-                    picked[:, t, :], a_sb[t][:].indirect(p1[:, starts[c] // 16 : (starts[c] + width) // 16])
-                )
-                nc.scalar.activation(picked[:, t, :], picked[:, t, :], ACT.Tanh)
-            ga.append(picked)
+        def make_z(t, cols):
+            entries = p1[:, cols.start // 16 : cols.stop // 16]
+            nc.vector.tensor_tensor(y[:, t, cols], x_sb[t][:].indirect(entries), gb[:, t, cols], ALU.subtract)
+            nc.vector.tensor_tensor(z_bf[:, t, cols], y[:, t, cols], gd[:, t, cols], ALU.max)
 
         out_v = out.rearrange("(n p) j -> p n j", p=P)
         last = len(CHUNKS) - 1
 
-        def combine(c):
-            cols = slice(starts[c], starts[c] + CHUNKS[c])
-            for t in range(4):
-                nc.vector.scalar_tensor_tensor(
-                    ga[c][:, t, :], ga[c][:, t, :], gain_sb[:, t, 0:1], gb[:, t, cols], ALU.mult, ALU.subtract
-                )
-
-        def round_z(c):
+        def project(c, cols):
             width = CHUNKS[c]
-            cols = slice(starts[c], starts[c] + width)
-            z_bf = keep.tile([P, 4, width], BF16, name="z_bf%d" % c)
-            nc.vector.tensor_tensor(z_bf[:], ga[c][:], gd[:, :, cols], ALU.max)
-            return z_bf
-
-        def weave_z(c, z_bf):
-            grouped = keep.tile([P, PACK * CHUNKS[c]], BF16, name="z_il%d" % c, align_bytes=64)
-            src = z_bf[:].rearrange("p t j -> p j t")
-            dst = grouped[:].rearrange("p (j t) -> p j t", t=4)
-            if c == 0:
-                nc.scalar.copy(dst, src)
-            else:
-                nc.vector.tensor_copy(dst, src)
-            return grouped
-
-        def project(c, grouped):
-            width = CHUNKS[c]
-            cols = slice(starts[c], starts[c] + width)
+            grouped = keep.tile([P, PACK * width], BF16, name="z_il%d" % c, align_bytes=64)
+            nc.vector.tensor_copy(
+                grouped[:].rearrange("p (c e t) -> p c t e", e=4, t=4),
+                z_bf[:, :, cols].rearrange("p t (c e) -> p c t e", e=4),
+            )
             z_codes, z_plane = quantize(grouped, width, "z%d" % c)
             per_bank = min(BANK // width, 3)
             staged = big.tile([P, N // P, width], F32, name="staged", tag=("slot_b", "slot_c", "slot_d")[c], align_bytes=64)
@@ -281,14 +256,11 @@ def tile_list_tube_acceptance_features_kernel(
                     nc.scalar.copy(staged[:, n0 : n0 + per_bank, :], acc[:])
                 nc.sync.dma_start(out_v[:, n0 : n0 + per_bank, cols], staged[:, n0 : n0 + per_bank, :])
 
-        combine(0)
-        grouped = weave_z(0, round_z(0))
-        combine(1)
-        w4_codes, w4_plane = quantize(w4_bf, N, "w4")
-        for c in range(1, len(CHUNKS)):
-            project(c - 1, grouped)
-            z_bf = round_z(c)
+        for t in range(3):
+            make_z(t, slice(0, PJ))
+        chunk_cols = [slice(sum(CHUNKS[:c]), sum(CHUNKS[: c + 1])) for c in range(len(CHUNKS))]
+        make_z(3, chunk_cols[0])
+        for c in range(len(CHUNKS)):
             if c < last:
-                combine(c + 1)
-            grouped = weave_z(c, z_bf)
-        project(last, grouped)
+                make_z(3, chunk_cols[c + 1])
+            project(c, chunk_cols[c])

from contextlib import ExitStack

import concourse.mybir as mybir

K, K2, T, S, PJ, H, N = 1024, 512, 4096, 1024, 512, 512, 768
FLOPS = 2 * (K * H * S + 2 * K2 * H * S + H * N * PJ)

F32 = mybir.dt.float32
BF16 = mybir.dt.bfloat16
I32 = mybir.dt.int32
U32 = mybir.dt.uint32
U16 = mybir.dt.uint16
U8 = mybir.dt.uint8
FP8X4 = mybir.dt.float8_e4m3fn_x4
FP4X4 = mybir.dt.float4_e2m1fn_x4
ALU = mybir.AluOpType
ACT = mybir.ActivationFunctionType

P = 128
PACK = 4
BANK = 512
CHUNKS = (128, 256, 128)


def tile_list_tube_acceptance_features_kernel(
    tc, tab_words, tab_scales, tab2_words, tab2_scales, tab3_words, tab3_scales, offs, offs2, offs3,
    pos1, pos2, pos3, w1, w2_words, w2_scales, w3, w4, setting, gain, out,
):
    nc = tc.nc
    with ExitStack() as ctx:
        keep = ctx.enter_context(tc.tile_pool(name="keep", bufs=1))
        big = ctx.enter_context(tc.tile_pool(name="big", bufs=1))
        psum = ctx.enter_context(tc.psum_pool(name="psum", bufs=8))

        def load_list(src, name):
            lst = keep.tile([P, src.shape[1]], U16, name=name)
            nc.sync.dma_start(lst[:], src)
            return lst

        def load_scale_rows(scales, name, tag):
            passes = scales.shape[0]
            first = P - 16 * passes
            rows = big.tile([P, T], U8, name=name, tag=tag, align_bytes=64)
            for a in range(passes):
                nc.sync.dma_start(rows[first + a : P : passes, :].bitcast(I32), scales[a].bitcast(I32))
            nc.vector.memset(rows[0:first, :].bitcast(I32), 0)
            return rows

        def place_scale_rows(picked, passes, name):
            first = P - 16 * passes
            plane = keep.tile([P, passes, S], U8, name=name, align_bytes=64)
            nc.vector.memset(plane[:].rearrange("p a s -> p (a s)").bitcast(I32), 0)
            for q in range(4):
                nc.sync.dma_start(
                    plane[32 * q : 32 * q + 4, :, :].bitcast(I32),
                    picked[first + 4 * passes * q : first + 4 * passes * (q + 1), :].bitcast(I32),
                )
            return plane

        def load_words(words, name, tag):
            win = big.tile([P, T], I32, name=name, tag=tag, align_bytes=64)
            nc.sync.dma_start(win[:], words.rearrange("p t i -> p (t i)").bitcast(I32))
            return win

        def gather_scales(rows, lst, name):
            picked = keep.tile([P, S], U8, name=name, align_bytes=64)
            nc.vector.tensor_copy(picked[:], rows[:].indirect(lst[:]))
            return picked

        def gather_words(win, lst, name):
            halves = []
            for h in range(S // BANK):
                picked = keep.tile([P, BANK], U32, name="picked", tag="%s_%d" % (name, h), align_bytes=64)
                nc.vector.tensor_copy(picked[:], win[:].bitcast(U32).indirect(lst[:, 32 * h : 32 * h + 32]))
                halves.append(picked)
            return halves

        def load_weight(rows, name, tag):
            raw = big.tile([P, PACK, H], F32, name=name, tag=tag, align_bytes=64)
            nc.sync.dma_start(raw[:], rows.rearrange("(p j) c -> p j c", j=PACK))
            return raw

        def round_weight(raw, tag):
            grouped = keep.tile([P, PACK * H], BF16, tag=tag, align_bytes=64)
            nc.scalar.copy(
                grouped[:].rearrange("p (t m j) -> p m j t", t=4, j=4),
                raw[:].rearrange("p j (m t) -> p m j t", t=4),
            )
            return grouped

        def quantize(grouped, width, name):
            codes = keep.tile([P, width], U32, name=name + "_codes", align_bytes=64)
            plane = keep.tile([P, width], U8, name=name + "_plane", align_bytes=64)
            c0 = 0
            while c0 < width:
                c1 = min(c0 + 512, width)
                nc.vector.quantize_mx(
                    out=codes[:, c0:c1].bitcast(FP8X4), scales=plane[:, c0:c1], in_=grouped[:, PACK * c0 : PACK * c1]
                )
                c0 = c1
            return codes, plane

        w2s_rows = keep.tile([P, H], U8)
        nc.vector.memset(w2s_rows[:].bitcast(I32), 0)
        l2 = load_list(offs2, "l2")
        s2_rows = load_scale_rows(tab2_scales, "s2_rows", "slot_a")
        l3 = load_list(offs3, "l3")
        s3_rows = load_scale_rows(tab3_scales, "s3_rows", "slot_b")
        l1 = load_list(offs, "l1")
        s1_rows = load_scale_rows(tab_scales, "s1_rows", "slot_c")
        w3_raw = load_weight(w3, "w3_raw", "slot_d")
        for q in range(4):
            nc.sync.dma_start(
                w2s_rows[32 * q : 32 * q + 4, :].bitcast(I32), w2_scales[0, 4 * q : 4 * q + 4, :].bitcast(I32)
            )
        w2_raw = keep.tile([P, H // 2], I32)
        nc.sync.dma_start(w2_raw[:], w2_words[0].bitcast(I32))
        p1 = load_list(pos1, "p1")
        win2 = load_words(tab2_words[0], "win2", "slot_e")
        p2 = load_list(pos2, "p2")
        p3 = load_list(pos3, "p3")

        warm_in = keep.tile([P, 1], F32)
        nc.vector.memset(warm_in[:], 0.0)
        warm_out = keep.tile([P, 1], F32)
        nc.scalar.activation(warm_out[:], warm_in[:], ACT.Tanh)

        g2s = place_scale_rows(gather_scales(s2_rows, l2, "pick2"), 1, "g2s")
        win3 = load_words(tab3_words[0], "win3", "slot_a")
        g3s = place_scale_rows(gather_scales(s3_rows, l3, "pick3"), 1, "g3s")
        w1_raw = [load_weight(w1[0:512, :], "w1_raw0", "slot_b")]
        g1s = place_scale_rows(gather_scales(s1_rows, l1, "pick1"), 2, "g1s")
        w1_raw.append(load_weight(w1[512:1024, :], "w1_raw1", "slot_c"))

        w2_codes = big.tile([P, 2 * H], U8, tag="slot_f", align_bytes=64)
        nc.vector.tensor_copy(
            w2_codes[:].rearrange("p (t m e) -> p t m e", t=4, e=2),
            w2_raw[:].bitcast(U8).rearrange("p (m t e) -> p t m e", t=4, e=2),
        )
        w2_plane = keep.tile([P, H], U8, align_bytes=64)
        nc.vector.tensor_copy(
            w2_plane[:].rearrange("p (t m) -> p t m", t=4),
            w2s_rows[:].rearrange("p (m t) -> p t m", t=4),
        )
        w3_bf = round_weight(w3_raw, "w3_bf")
        win1 = [load_words(tab_words[0], "win1_0", "slot_d")]
        w3_codes, w3_plane = quantize(w3_bf, H, "w3")
        g2w = gather_words(win2, l2, "g2w")

        win1.append(load_words(tab_words[1], "win1_1", "slot_e"))

        b_sb = [big.tile([P, S], F32, name="b_sb%d" % t, tag="slot_g%d" % t) for t in range(4)]
        for t in range(4):
            for h in range(2):
                cols = slice(BANK * h, BANK * (h + 1))
                acc = psum.tile([P, BANK], F32, tag="acc")
                nc.tensor.matmul_mx(
                    out=acc[:], lhsT=w2_codes[:, 2 * P * t : 2 * P * (t + 1)].bitcast(FP4X4),
                    lhsT_scale=w2_plane[:, P * t : P * (t + 1)],
                    rhs=g2w[h][:].bitcast(FP8X4), rhs_scale=g2s[:, 0, cols], start=True, stop=True,
                )
                nc.scalar.copy(b_sb[t][:, cols], acc[:])

        w4_raw = big.tile([P, 4, N], F32, tag="slot_f", align_bytes=64)
        nc.sync.dma_start(w4_raw[:], w4.rearrange("(p t) n -> p t n", t=4))

        g3w = gather_words(win3, l3, "g3w")

        gbd = big.tile([P, 8, PJ], F32, tag="slot_a", align_bytes=64)
        gb = gbd[:, 0:4, :]
        gd = gbd[:, 4:8, :]
        for t in range(4):
            nc.vector.tensor_copy(gb[:, t, :], b_sb[t][:].indirect(p2[:]))
        gain_sb = keep.tile([P, 4], F32, tag="w3_bf", align_bytes=64)
        nc.sync.dma_start(gain_sb[:], gain.rearrange("(p t) -> p t", t=4))
        setting_sb = [big.tile([P, S], F32, name="setting%d" % t, tag="slot_g%d" % t) for t in range(4)]
        for t in range(4):
            nc.sync.dma_start(setting_sb[t][:], setting.rearrange("(p t) j -> t p j", t=4)[t])

        d_sb = [keep.tile([P, S], F32, name="d_sb%d" % t) for t in range(4)]
        for t in range(4):
            for h in range(2):
                cols = slice(BANK * h, BANK * (h + 1))
                acc = psum.tile([P, BANK], F32, tag="acc")
                nc.tensor.matmul_mx(
                    out=acc[:], lhsT=w3_codes[:, P * t : P * (t + 1)].bitcast(FP8X4),
                    lhsT_scale=w3_plane[:, P * t : P * (t + 1)],
                    rhs=g3w[h][:].bitcast(FP8X4), rhs_scale=g3s[:, 0, cols], start=True, stop=True,
                )
                nc.scalar.copy(d_sb[t][:, cols], acc[:])
        w1_bf = [round_weight(w1_raw[a], "g3w_%d" % (1 - a)) for a in range(2)]
        for t in range(4):
            nc.vector.tensor_copy(gd[:, t, :], d_sb[t][:].indirect(p3[:]))

        w1_q = [quantize(w1_bf[a], H, "w1_%d" % a) for a in range(2)]
        accs = [[psum.tile([P, BANK], F32, tag="acc", name="acc") for t in range(4)] for h in range(2)]
        for a in range(2):
            g1w = gather_words(win1[a], l1, "g1w%d" % a)
            codes, plane = w1_q[a]
            for h in range(2):
                for t in range(4):
                    nc.tensor.matmul_mx(
                        out=accs[h][t][:], lhsT=codes[:, P * t : P * (t + 1)].bitcast(FP8X4),
                        lhsT_scale=plane[:, P * t : P * (t + 1)],
                        rhs=g1w[h][:].bitcast(FP8X4),
                        rhs_scale=g1s[:, a, BANK * h : BANK * (h + 1)],
                        start=(a == 0), stop=(a == 1),
                    )
        w4_bf = keep.tile([P, PACK * N], BF16, align_bytes=64)
        nc.scalar.copy(
            w4_bf[:].rearrange("p (c e t) -> p c t e", e=4, t=4), w4_raw[:].rearrange("p t (c e) -> p c t e", e=4)
        )
        w4_codes, w4_plane = quantize(w4_bf, N, "w4")

        x_sb = [keep.tile([P, S], F32, name="x_sb%d" % t) for t in range(4)]
        for t in range(4):
            for h in range(2):
                cols = slice(BANK * h, BANK * (h + 1))
                nc.vector.tensor_tensor(x_sb[t][:, cols], accs[h][t][:], setting_sb[t][:, cols], ALU.add)
                nc.scalar.activation(x_sb[t][:, cols], x_sb[t][:, cols], ACT.Tanh)
                nc.scalar.activation(x_sb[t][:, cols], x_sb[t][:, cols], ACT.Copy, scale=gain_sb[:, t : t + 1])

        y = keep.tile([P, 4, PJ], F32)
        z_bf = keep.tile([P, 4, PJ], BF16)

        def make_z(t, cols):
            entries = p1[:, cols.start // 16 : cols.stop // 16]
            nc.vector.tensor_tensor(y[:, t, cols], x_sb[t][:].indirect(entries), gb[:, t, cols], ALU.subtract)
            nc.vector.tensor_tensor(z_bf[:, t, cols], y[:, t, cols], gd[:, t, cols], ALU.max)

        out_v = out.rearrange("(n p) j -> p n j", p=P)
        last = len(CHUNKS) - 1

        def project(c, cols):
            width = CHUNKS[c]
            grouped = keep.tile([P, PACK * width], BF16, name="z_il%d" % c, align_bytes=64)
            nc.vector.tensor_copy(
                grouped[:].rearrange("p (c e t) -> p c t e", e=4, t=4),
                z_bf[:, :, cols].rearrange("p t (c e) -> p c t e", e=4),
            )
            z_codes, z_plane = quantize(grouped, width, "z%d" % c)
            per_bank = min(BANK // width, 3)
            staged = big.tile([P, N // P, width], F32, name="staged", tag=("slot_b", "slot_c", "slot_d")[c], align_bytes=64)
            for n0 in range(0, N // P, per_bank):
                acc = psum.tile([P, per_bank, width], F32, tag="acc")
                for i in range(per_bank):
                    n = n0 + i
                    nc.tensor.matmul_mx(
                        out=acc[:, i, :], lhsT=w4_codes[:, P * n : P * (n + 1)].bitcast(FP8X4),
                        lhsT_scale=w4_plane[:, P * n : P * (n + 1)],
                        rhs=z_codes[:].bitcast(FP8X4), rhs_scale=z_plane[:], start=True, stop=True,
                    )
                if c == last and (n0 // per_bank) % 2 == 1:
                    nc.vector.tensor_copy(staged[:, n0 : n0 + per_bank, :], acc[:])
                else:
                    nc.scalar.copy(staged[:, n0 : n0 + per_bank, :], acc[:])
                nc.sync.dma_start(out_v[:, n0 : n0 + per_bank, cols], staged[:, n0 : n0 + per_bank, :])

        for t in range(3):
            make_z(t, slice(0, PJ))
        chunk_cols = [slice(sum(CHUNKS[:c]), sum(CHUNKS[: c + 1])) for c in range(len(CHUNKS))]
        make_z(3, chunk_cols[0])
        for c in range(len(CHUNKS)):
            if c < last:
                make_z(3, chunk_cols[c + 1])
            project(c, chunk_cols[c])
